import numpy as np
import ml_dtypes


def mxq(x, axis, fmt="e4m3"):
    dtype, down = {"e4m3": (ml_dtypes.float8_e4m3fn, 7), "e5m2": (ml_dtypes.float8_e5m2, 14)}[fmt]
    v = np.moveaxis(np.asarray(x, np.float32).astype(ml_dtypes.bfloat16).astype(np.float64), axis, -1)
    blocks = v.reshape(v.shape[:-1] + (-1, 32))
    amax = np.abs(blocks).max(-1, keepdims=True)
    byte = np.maximum(np.where(amax > 0, np.frexp(amax)[1] - 1 + 127, 0) - down, 1)
    scale = np.exp2(byte - 127.0)
    codes = (blocks / scale).astype(np.float32).astype(dtype).astype(np.float64)
    return np.moveaxis((codes * scale).reshape(v.shape), -1, axis)


WIDE = False


def mx_kscale(k):
    if not WIDE:
        return np.ones(k)
    levels = np.array([10, -10, 5, -5, 0])
    if k % 512:
        return np.exp2(np.random.permutation(np.resize(levels, k // 32))).repeat(32)
    a = np.empty((k // 512, 16))
    for p in range(k // 512):
        a[p, :8] = np.random.permutation(np.resize(levels, 8))
        for g in range(8):
            far = levels[np.abs(levels - a[p, g]) >= 10]
            a[p, g + 8] = far[np.random.randint(len(far))]
    return np.exp2(a.ravel()).repeat(32)


def f64(x):
    return np.asarray(x).astype(np.float64)


def striped(idx):
    return np.tile(idx.reshape(-1, 16).T, (8, 1)).astype(np.uint16)


def unstriped(offs):
    return offs[:16].T.reshape(-1).astype(np.int64)


def pack_weight(w):
    k, n = w.shape
    w = f64(np.asarray(w, np.float32).astype(ml_dtypes.bfloat16)).reshape(k // 32, 32, n)
    amax = np.abs(w).max(1)
    byte = np.clip(np.where(amax > 0, np.frexp(amax)[1] - 1 + 127 - 7, 1), 1, 254)
    scaled = (w * np.exp2(127.0 - byte)[:, None, :]).reshape(k, n).astype(np.float32)
    words = np.ascontiguousarray(scaled.reshape(k // 512, 128, 4, n).transpose(0, 1, 3, 2)).astype(ml_dtypes.float8_e4m3fn).view(np.uint8)
    return words, np.ascontiguousarray(byte.astype(np.uint8).reshape(k // 512, 16, n))


def unpack_weight(words, scales):
    g, p, n, _ = words.shape
    vals = np.ascontiguousarray(words).view(ml_dtypes.float8_e4m3fn).astype(np.float64) * np.repeat(np.exp2(scales.astype(np.float64) - 127.0), 8, axis=1)[..., None]
    return vals.transpose(0, 1, 3, 2).reshape(g * 512, n)


K, T, S, D, V, H, N = 1024, 2048, 1024, 2, 512, 512, 128
P = 2 ** 7


def setup_inputs():
    n = np.random.standard_normal
    s = mx_kscale(K)[:, None]
    u = mx_kscale(H)
    packed_xT = pack_weight(n((K, T)) * s)
    return {
        "x_words": packed_xT[0],
        "x_scales": packed_xT[1],
        "w1": (n((K, H)) / np.sqrt(K) / s * u).astype(np.float32),
        "w2": (n((H, N)) / np.sqrt(H) / u[:, None]).astype(np.float32),
        "gate": (np.tile(np.random.uniform(0.2, 1.0, (D, 1, V)) / np.sqrt(D), (1, P, 1))).astype(np.float32),
        "offs": striped(np.random.permutation(T)[:S]),
        "cen": striped(np.random.permutation(S)[:V]),
        "pos1": striped(np.random.permutation(S)[:V]),
        "pos2": striped(np.random.permutation(S)[:V]),
    }


def reference(x_words, x_scales, w1, w2, gate, offs, cen, pos1, pos2):
    xq = unpack_weight(x_words, x_scales)[:, unstriped(offs)]
    h = mxq(f64(w1), 0, "e4m3").T @ xq
    z = h[:, unstriped(cen)] - (h[:, unstriped(pos1)] * f64(gate)[0, :1] + h[:, unstriped(pos2)] * f64(gate)[1, :1])
    return mxq(f64(w2), 0, "e4m3").T @ mxq(z, 0, "e4m3")

@@ -1,0 +1,231 @@
+from contextlib import ExitStack
+
+import concourse.mybir as mybir
+from concourse.masks import make_identity
+
+K, T, S, V, H, N = 1024, 2048, 1024, 512, 512, 128
+FLOPS = 2 * K * H * S + 2 * H * N * V
+
+F32 = mybir.dt.float32
+BF16 = mybir.dt.bfloat16
+I32 = mybir.dt.int32
+U32 = mybir.dt.uint32
+U16 = mybir.dt.uint16
+U8 = mybir.dt.uint8
+FP8X4 = mybir.dt.float8_e4m3fn_x4
+MULT = mybir.AluOpType.mult
+
+P = 128
+PACK = 4
+K_PASS = P * PACK
+PASSES = K // K_PASS
+TILES = H // P
+BANK = 512
+
+
+def tile_picked_lapl_none_p_kernel(tc, x_words, x_scales, w1, w2, gate, offs, cen, pos1, pos2, out):
+    nc = tc.nc
+    with ExitStack() as ctx:
+        keep = ctx.enter_context(tc.tile_pool(name="keep", bufs=1))
+        psum = ctx.enter_context(tc.psum_pool(name="psum", bufs=1))
+
+        def entries(lst, a, b):
+            return lst[:, a // 16 : b // 16]
+
+        offs_sb = keep.tile([P, S // 16], U16, name="offs_sb")
+        nc.sync.dma_start(offs_sb[:], offs)
+        lists = [keep.tile([P, V // 16], U16, name=name) for name in ("cen_sb", "pos1_sb", "pos2_sb")]
+        nc.sync.dma_start(lists[0][:], cen)
+        nc.sync.dma_start(lists[1][:], pos1)
+
+        scale_win = keep.tile([P, T], U8, name="scale_win", tag="first", align_bytes=64)
+        nc.gpsimd.memset(scale_win[:].bitcast(I32), 0)
+        for q in range(4):
+            nc.sync.dma_start(
+                scale_win[32 * q : 32 * q + 4 * PASSES, :].bitcast(I32),
+                x_scales[:, 4 * q : 4 * q + 4, :].bitcast(I32),
+            )
+
+        word_win = [keep.tile([P, T], U32, name=f"word_win{z}", align_bytes=64) for z in range(PASSES)]
+
+        def load_words(z):
+            nc.sync.dma_start(word_win[z][:].bitcast(I32), x_words[z].rearrange("p n r -> p (n r)").bitcast(I32))
+
+        w1_raw = {}
+
+        def load_w1(z, t0, t1):
+            raw = keep.tile([P, PACK, (t1 - t0) * P], F32, name=f"w1_raw{z}_{t0}", tag=f"w1_raw{z}_{t0}", align_bytes=64)
+            nc.sync.dma_start(
+                raw[:], w1[z * K_PASS : (z + 1) * K_PASS, t0 * P : t1 * P].rearrange("(p j) c -> p j c", j=PACK)
+            )
+            for t in range(t0, t1):
+                w1_raw[z, t] = raw[:, :, (t - t0) * P : (t - t0 + 1) * P]
+
+        load_words(0)
+        load_w1(0, 0, 1)
+        load_words(1)
+        load_w1(1, 0, 1)
+        nc.sync.dma_start(lists[2][:], pos2)
+        for z in range(PASSES):
+            load_w1(z, 1, 2)
+        gate_sb = keep.tile([P, 2, V], F32, name="gate_sb")
+        nc.sync.dma_start(gate_sb[:], gate.rearrange("d p v -> p d v"))
+        for z in range(PASSES):
+            load_w1(z, 2, 4)
+        w2_raw = keep.tile([P, PACK, N], F32, name="w2_raw")
+        nc.sync.dma_start(w2_raw[:], w2.rearrange("(p j) n -> p j n", j=PACK))
+
+        ident = keep.tile([P, P], F32, name="ident")
+        make_identity(nc, ident[:])
+
+        def interleave(dst, raw, copy=nc.scalar.copy):
+            copy(
+                dst.rearrange("p (c i j) -> p c j i", i=4, j=PACK),
+                raw.rearrange("p j (c i) -> p c j i", i=4),
+            )
+
+        def quantize(codes, scales, grouped):
+            nc.vector.quantize_mx(out=codes.bitcast(FP8X4), scales=scales, in_=grouped)
+
+        codes_all = [keep.tile([P, n * PASSES * P], U32, name=f"w1_codes{t}", align_bytes=64) for t, n in enumerate((1, 1, 2))]
+        scales_all = [keep.tile([P, n * PASSES * P], U8, name=f"w1_scales{t}", align_bytes=64) for t, n in enumerate((1, 1, 2))]
+        w1_codes = [codes_all[0][:], codes_all[1][:], codes_all[2][:, :256], codes_all[2][:, 256:]]
+        w1_scales = [scales_all[0][:], scales_all[1][:], scales_all[2][:, :256], scales_all[2][:, 256:]]
+
+        x_scale = keep.tile([P, S], U8, name="x_scale", align_bytes=64)
+        nc.vector.tensor_copy(x_scale[:], scale_win[:].indirect(offs_sb[:]))
+        x_first = keep.tile([P, S], U32, name="x_first", tag="first", align_bytes=64)
+        nc.vector.tensor_copy(x_first[:], word_win[0][:].indirect(offs_sb[:]))
+
+        def prepare_first(z):
+            grouped = keep.tile([P, K_PASS], BF16, name=f"w1_first{z}", tag=f"w1_first{z}", align_bytes=64)
+            interleave(grouped[:], w1_raw[z, 0])
+            quantize(w1_codes[0][:, z * P : (z + 1) * P], w1_scales[0][:, z * P : (z + 1) * P], grouped[:])
+
+        pieces = [(0, 512), (512, 768), (768, 1024)]
+        x_low = keep.tile([P, BANK], U32, name="x_low", align_bytes=64)
+        x_later = []
+
+        def words(z, a, b):
+            if z == 0:
+                return x_first[:, a:b]
+            return x_low[:, a:b] if b <= BANK else x_later[0][:, a - BANK : b - BANK]
+
+        h = [keep.tile([P, S], F32, name=f"h{t}", tag=f"h{t}", align_bytes=64) for t in range(TILES)]
+
+        def bank_tile(n):
+            return psum.tile([P, BANK], F32, name="bank", tag=f"bank{n}")
+
+        def project(t, a, b, n):
+            acc = bank_tile(n)
+            for z in range(PASSES):
+                nc.tensor.matmul_mx(
+                    out=acc[:, : b - a],
+                    lhsT=w1_codes[t][:, z * P : (z + 1) * P].bitcast(FP8X4),
+                    lhsT_scale=w1_scales[t][:, z * P : (z + 1) * P],
+                    rhs=words(z, a, b).bitcast(FP8X4),
+                    rhs_scale=x_scale[4 * z :, a:b],
+                    start=(z == 0),
+                    stop=(z == PASSES - 1),
+                )
+            nc.scalar.copy(h[t][:, a:b], acc[:, : b - a])
+
+        prepare_first(0)
+        for n, (a, b) in enumerate(pieces):
+            nc.vector.tensor_copy(words(1, a, b), word_win[1][:].indirect(entries(offs_sb, a, b)))
+            if n == 0:
+                prepare_first(1)
+                x_later.append(keep.tile([P, BANK], U32, name="x_high", tag="w1_first1", align_bytes=64))
+            project(0, a, b, n)
+
+        neg_gate = [keep.tile([P, V], F32, name=f"neg_gate{d}") for d in range(2)]
+
+        z_rows = keep.tile([P, V // P, H], BF16, name="z_rows", tag="w1_raw1_2", align_bytes=64)
+
+        def prepare(ts, banks, tag, copy):
+            grouped = keep.tile([P, len(ts), PASSES, K_PASS], BF16, name="w1_grouped", tag=tag, align_bytes=64)
+            for n, t in enumerate(ts):
+                for z in range(PASSES):
+                    interleave(grouped[:, n, z, :], w1_raw[z, t], copy)
+            quantize(codes_all[min(ts[0], 2)][:], scales_all[min(ts[0], 2)][:], grouped[:].rearrange("p n z c -> p (n z c)"))
+            for n, t in enumerate(ts):
+                for half in range(2):
+                    project(t, half * BANK, (half + 1) * BANK, banks[2 * n + half])
+
+        def look_up(t, a, b, n, between=()):
+            width = b - a
+            bank = bank_tile(n)
+            for d in range(3):
+                if t == 1 and d == 2:
+                    term = both[:, 1, :]
+                elif t == 1 and d == 1:
+                    both = keep.tile([P, 2, width], F32, name="both", tag="term1_0_1", align_bytes=64)
+                    term = both[:, 0, :]
+                else:
+                    term = keep.tile([P, width], F32, name="term", tag=f"term{t}_{a}_{d}", align_bytes=64)[:]
+                window = h[t][:].indirect(entries(lists[d], a, b))
+                if d == 0:
+                    nc.vector.tensor_copy(term, window)
+                else:
+                    nc.vector.tensor_tensor(term, window, neg_gate[d - 1][:, a:b], MULT)
+                if d < len(between):
+                    prepare(*between[d])
+                for c in range(0, width, P):
+                    nc.tensor.matmul(
+                        bank[:, c : c + P], term[:, c : c + P], ident[:], is_transpose=True,
+                        start=(d == 0 and c == 0), stop=(d == 2 and c == width - P),
+                    )
+            nc.scalar.copy(
+                z_rows[:, a // P : b // P, :].rearrange("v c (u p e) -> v c u p e", u=2, e=2)[:, :, :, 32 * t : 32 * t + 32, :],
+                bank[:, :width].rearrange("v (c p u e) -> v c u p e", p=32, u=2, e=2),
+            )
+
+        def turn_back(a, b, n, tag):
+            width = b - a
+            bank = bank_tile(n)
+            pairs = z_rows[:, a // P : b // P, :].rearrange("v c i -> v (c i)").bitcast(F32)
+            for c in range(0, 2 * width, P):
+                nc.tensor.transpose(bank[:, c : c + P], pairs[:, c : c + P], ident[:])
+            grouped = keep.tile([P, PACK * width], BF16, name="z_grouped", tag=tag, align_bytes=64)
+            nc.scalar.copy(
+                grouped[:].bitcast(F32).rearrange("p (c v u) -> p c v u", v=P, u=2),
+                bank[:, : 2 * width].rearrange("p (c u v) -> p c v u", v=P, u=2),
+            )
+            return grouped
+
+        def finish(grouped, a, b, n, copy_out, tag):
+            width = b - a
+            codes = keep.tile([P, width], U32, name=f"z_codes{a}", tag=tag, align_bytes=64)
+            scales = keep.tile([P, width], U8, name=f"z_scales{a}", align_bytes=64)
+            quantize(codes[:], scales[:], grouped[:])
+            acc = bank_tile(n)
+            nc.tensor.matmul_mx(
+                out=acc[:, :width], lhsT=w2_codes[:].bitcast(FP8X4), lhsT_scale=w2_scales[:],
+                rhs=codes[:].bitcast(FP8X4), rhs_scale=scales[:], start=True, stop=True,
+            )
+            result = keep.tile([P, width], F32, name=f"result{a}")
+            copy_out(result[:], acc[:, :width])
+            nc.sync.dma_start(out[:, a:b], result[:])
+
+        prepare([1], (3, 0), "term0_0_0", nc.vector.tensor_copy)
+        for d in range(2):
+            nc.scalar.mul(neg_gate[d][:], gate_sb[:, d, :], -1.0)
+        look_up(0, 0, V, 4)
+        look_up(1, 0, V, 5, [([2, 3], (1, 2, 3, 0), "term1_0_1", nc.scalar.copy)])
+        look_up(2, 0, 256, 6)
+        w2_grouped = keep.tile([P, PACK * N], BF16, name="w2_grouped", tag="w2_grouped", align_bytes=64)
+        interleave(w2_grouped[:], w2_raw[:])
+        look_up(3, 0, 256, 7)
+        look_up(2, 256, 384, 4)
+        first = turn_back(0, 256, 1, "first_grouped")
+        look_up(3, 256, 384, 7)
+        look_up(2, 384, 512, 1)
+        second = turn_back(256, 384, 2, "second")
+        look_up(3, 384, 512, 7)
+        w2_codes = keep.tile([P, N], U32, name="w2_codes", tag="h3", align_bytes=64)
+        w2_scales = keep.tile([P, N], U8, name="w2_scales", align_bytes=64)
+        quantize(w2_codes[:], w2_scales[:], w2_grouped[:])
+        finish(first, 0, 256, 0, nc.vector.tensor_copy, "w2_grouped")
+        third = turn_back(384, 512, 3, "third")
+        finish(second, 256, 384, 6, nc.vector.tensor_copy, "codes1")
+        finish(third, 384, 512, 5, nc.vector.tensor_copy, "codes2")

@@ -87,10 +87,10 @@ def tile_picked_lapl_none_p_kernel(tc, x_words, x_scales, w1, w2, gate, offs, ce
         def quantize(codes, scales, grouped):
             nc.vector.quantize_mx(out=codes.bitcast(FP8X4), scales=scales, in_=grouped)
 
-        codes_all = [keep.tile([P, n * PASSES * P], U32, name=f"w1_codes{t}", align_bytes=64) for t, n in enumerate((1, 1, 2))]
-        scales_all = [keep.tile([P, n * PASSES * P], U8, name=f"w1_scales{t}", align_bytes=64) for t, n in enumerate((1, 1, 2))]
-        w1_codes = [codes_all[0][:], codes_all[1][:], codes_all[2][:, :256], codes_all[2][:, 256:]]
-        w1_scales = [scales_all[0][:], scales_all[1][:], scales_all[2][:, :256], scales_all[2][:, 256:]]
+        codes_all = [keep.tile([P, n * PASSES * P], U32, name=f"w1_codes{t}", align_bytes=64) for t, n in enumerate((1, 1))]
+        scales_all = [keep.tile([P, n * PASSES * P], U8, name=f"w1_scales{t}", align_bytes=64) for t, n in enumerate((1, 1, 1, 1))]
+        w1_codes = codes_all
+        w1_scales = scales_all
 
         x_scale = keep.tile([P, S], U8, name="x_scale", align_bytes=64)
         nc.vector.tensor_copy(x_scale[:], scale_win[:].indirect(offs_sb[:]))
@@ -138,7 +138,8 @@ def tile_picked_lapl_none_p_kernel(tc, x_words, x_scales, w1, w2, gate, offs, ce
                 x_later.append(keep.tile([P, BANK], U32, name="x_high", tag="w1_first1", align_bytes=64))
             project(0, a, b, n)
 
-        neg_gate = [keep.tile([P, V], F32, name=f"neg_gate{d}") for d in range(2)]
+        neg_gate = keep.tile([P, 2, V], F32, name="neg_gate")
+        nc.scalar.mul(neg_gate[:], gate_sb[:], -1.0)
 
         z_rows = keep.tile([P, V // P, H], BF16, name="z_rows", tag="w1_raw1_2", align_bytes=64)
 
@@ -147,34 +148,35 @@ def tile_picked_lapl_none_p_kernel(tc, x_words, x_scales, w1, w2, gate, offs, ce
             for n, t in enumerate(ts):
                 for z in range(PASSES):
                     interleave(grouped[:, n, z, :], w1_raw[z, t], copy)
-            quantize(codes_all[min(ts[0], 2)][:], scales_all[min(ts[0], 2)][:], grouped[:].rearrange("p n z c -> p (n z c)"))
+            if ts[0] > 1:
+                codes_all.append(keep.tile([P, PASSES * P], U32, name="late_codes", tag=("h0" if ts[0] == 2 else "term1_0_0"), align_bytes=64))
+            quantize(codes_all[ts[0]][:], scales_all[ts[0]][:], grouped[:].rearrange("p n z c -> p (n z c)"))
             for n, t in enumerate(ts):
                 for half in range(2):
                     project(t, half * BANK, (half + 1) * BANK, banks[2 * n + half])
 
-        def look_up(t, a, b, n, between=()):
+        ring = keep.tile([P, 6 * P], F32, name="ring", align_bytes=64)
+
+        def look_up(t, a, b, n, between=(), place=None):
             width = b - a
             bank = bank_tile(n)
             for d in range(3):
-                if t == 1 and d == 2:
-                    term = both[:, 1, :]
-                elif t == 1 and d == 1:
-                    both = keep.tile([P, 2, width], F32, name="both", tag="term1_0_1", align_bytes=64)
-                    term = both[:, 0, :]
-                else:
+                if place is None:
                     term = keep.tile([P, width], F32, name="term", tag=f"term{t}_{a}_{d}", align_bytes=64)[:]
+                else:
+                    term = ring[:, place + d * width : place + (d + 1) * width]
                 window = h[t][:].indirect(entries(lists[d], a, b))
                 if d == 0:
                     nc.vector.tensor_copy(term, window)
                 else:
-                    nc.vector.tensor_tensor(term, window, neg_gate[d - 1][:, a:b], MULT)
-                if d < len(between):
-                    prepare(*between[d])
+                    nc.vector.tensor_tensor(term, window, neg_gate[:, d - 1, a:b], MULT)
                 for c in range(0, width, P):
                     nc.tensor.matmul(
                         bank[:, c : c + P], term[:, c : c + P], ident[:], is_transpose=True,
                         start=(d == 0 and c == 0), stop=(d == 2 and c == width - P),
                     )
+                if d < len(between):
+                    prepare(*between[d])
             nc.scalar.copy(
                 z_rows[:, a // P : b // P, :].rearrange("v c (u p e) -> v c u p e", u=2, e=2)[:, :, :, 32 * t : 32 * t + 32, :],
                 bank[:, :width].rearrange("v (c p u e) -> v c u p e", p=32, u=2, e=2),
@@ -208,20 +210,20 @@ def tile_picked_lapl_none_p_kernel(tc, x_words, x_scales, w1, w2, gate, offs, ce
             nc.sync.dma_start(out[:, a:b], result[:])
 
         prepare([1], (3, 0), "term0_0_0", nc.vector.tensor_copy)
-        for d in range(2):
-            nc.scalar.mul(neg_gate[d][:], gate_sb[:, d, :], -1.0)
         look_up(0, 0, V, 4)
-        look_up(1, 0, V, 5, [([2, 3], (1, 2, 3, 0), "term1_0_1", nc.scalar.copy)])
-        look_up(2, 0, 256, 6)
+        prepare([2], (1, 2), "term1_0_0", nc.scalar.copy)
+        look_up(1, 0, 384, 5, [([3], (3, 0), "term1_0_2", nc.scalar.copy)])
+        look_up(2, 0, 256, 6, place=0)
         w2_grouped = keep.tile([P, PACK * N], BF16, name="w2_grouped", tag="w2_grouped", align_bytes=64)
         interleave(w2_grouped[:], w2_raw[:])
-        look_up(3, 0, 256, 7)
-        look_up(2, 256, 384, 4)
+        look_up(3, 0, 256, 7, place=0)
         first = turn_back(0, 256, 1, "first_grouped")
-        look_up(3, 256, 384, 7)
-        look_up(2, 384, 512, 1)
+        look_up(2, 256, 384, 4, place=0)
+        look_up(3, 256, 384, 7, place=384)
         second = turn_back(256, 384, 2, "second")
-        look_up(3, 384, 512, 7)
+        look_up(1, 384, 512, 1, place=0)
+        look_up(2, 384, 512, 7, place=384)
+        look_up(3, 384, 512, 1, place=0)
         w2_codes = keep.tile([P, N], U32, name="w2_codes", tag="h3", align_bytes=64)
         w2_scales = keep.tile([P, N], U8, name="w2_scales", align_bytes=64)
         quantize(w2_codes[:], w2_scales[:], w2_grouped[:])

@@ -35,21 +35,21 @@ def tile_picked_lapl_none_p_kernel(tc, x_words, x_scales, w1, w2, gate, offs, ce
         offs_sb = keep.tile([P, S // 16], U16, name="offs_sb")
         nc.sync.dma_start(offs_sb[:], offs)
         lists = [keep.tile([P, V // 16], U16, name=name) for name in ("cen_sb", "pos1_sb", "pos2_sb")]
-        nc.sync.dma_start(lists[0][:], cen)
+        word_win = [keep.tile([P, T], U32, name=f"word_win{z}", align_bytes=64) for z in range(PASSES)]
+
+        def load_words(z):
+            nc.sync.dma_start(word_win[z][:].bitcast(I32), x_words[z].rearrange("p n r -> p (n r)").bitcast(I32))
+
+        load_words(0)
         nc.sync.dma_start(lists[1][:], pos1)
 
-        scale_win = keep.tile([P, T], U8, name="scale_win", tag="first", align_bytes=64)
+        scale_win = keep.tile([P, T], U8, name="scale_win", align_bytes=64)
         nc.gpsimd.memset(scale_win[:].bitcast(I32), 0)
         for q in range(4):
             nc.sync.dma_start(
                 scale_win[32 * q : 32 * q + 4 * PASSES, :].bitcast(I32),
                 x_scales[:, 4 * q : 4 * q + 4, :].bitcast(I32),
             )
-
-        word_win = [keep.tile([P, T], U32, name=f"word_win{z}", align_bytes=64) for z in range(PASSES)]
-
-        def load_words(z):
-            nc.sync.dma_start(word_win[z][:].bitcast(I32), x_words[z].rearrange("p n r -> p (n r)").bitcast(I32))
 
         w1_raw = {}
 
@@ -61,11 +61,11 @@ def tile_picked_lapl_none_p_kernel(tc, x_words, x_scales, w1, w2, gate, offs, ce
             for t in range(t0, t1):
                 w1_raw[z, t] = raw[:, :, (t - t0) * P : (t - t0 + 1) * P]
 
-        load_words(0)
         load_w1(0, 0, 1)
         load_words(1)
         load_w1(1, 0, 1)
         nc.sync.dma_start(lists[2][:], pos2)
+        nc.sync.dma_start(lists[0][:], cen)
         for z in range(PASSES):
             load_w1(z, 1, 2)
         gate_sb = keep.tile([P, 2, V], F32, name="gate_sb")
@@ -93,9 +93,9 @@ def tile_picked_lapl_none_p_kernel(tc, x_words, x_scales, w1, w2, gate, offs, ce
         w1_scales = scales_all
 
         x_scale = keep.tile([P, S], U8, name="x_scale", align_bytes=64)
-        nc.vector.tensor_copy(x_scale[:], scale_win[:].indirect(offs_sb[:]))
-        x_first = keep.tile([P, S], U32, name="x_first", tag="first", align_bytes=64)
+        x_first = keep.tile([P, S], U32, name="x_first", align_bytes=64)
         nc.vector.tensor_copy(x_first[:], word_win[0][:].indirect(offs_sb[:]))
+        nc.vector.tensor_copy(x_scale[:], scale_win[:].indirect(offs_sb[:]))
 
         def prepare_first(z):
             grouped = keep.tile([P, K_PASS], BF16, name=f"w1_first{z}", tag=f"w1_first{z}", align_bytes=64)

from contextlib import ExitStack

import concourse.mybir as mybir
from concourse.masks import make_identity

K, T, S, V, H, N = 1024, 2048, 1024, 512, 512, 128
FLOPS = 2 * K * H * S + 2 * H * N * V

F32 = mybir.dt.float32
BF16 = mybir.dt.bfloat16
I32 = mybir.dt.int32
U32 = mybir.dt.uint32
U16 = mybir.dt.uint16
U8 = mybir.dt.uint8
FP8X4 = mybir.dt.float8_e4m3fn_x4
MULT = mybir.AluOpType.mult

P = 128
PACK = 4
K_PASS = P * PACK
PASSES = K // K_PASS
TILES = H // P
BANK = 512


def tile_picked_lapl_none_p_kernel(tc, x_words, x_scales, w1, w2, gate, offs, cen, pos1, pos2, out):
    nc = tc.nc
    with ExitStack() as ctx:
        keep = ctx.enter_context(tc.tile_pool(name="keep", bufs=1))
        psum = ctx.enter_context(tc.psum_pool(name="psum", bufs=1))

        def entries(lst, a, b):
            return lst[:, a // 16 : b // 16]

        offs_sb = keep.tile([P, S // 16], U16, name="offs_sb")
        nc.sync.dma_start(offs_sb[:], offs)
        lists = [keep.tile([P, V // 16], U16, name=name) for name in ("cen_sb", "pos1_sb", "pos2_sb")]
        word_win = [keep.tile([P, T], U32, name=f"word_win{z}", align_bytes=64) for z in range(PASSES)]

        def load_words(z):
            nc.sync.dma_start(word_win[z][:].bitcast(I32), x_words[z].rearrange("p n r -> p (n r)").bitcast(I32))

        load_words(0)
        nc.sync.dma_start(lists[1][:], pos1)

        scale_win = keep.tile([P, T], U8, name="scale_win", align_bytes=64)
        nc.gpsimd.memset(scale_win[:].bitcast(I32), 0)
        for q in range(4):
            nc.sync.dma_start(
                scale_win[32 * q : 32 * q + 4 * PASSES, :].bitcast(I32),
                x_scales[:, 4 * q : 4 * q + 4, :].bitcast(I32),
            )

        w1_raw = {}

        def load_w1(z, t0, t1):
            raw = keep.tile([P, PACK, (t1 - t0) * P], F32, name=f"w1_raw{z}_{t0}", tag=f"w1_raw{z}_{t0}", align_bytes=64)
            nc.sync.dma_start(
                raw[:], w1[z * K_PASS : (z + 1) * K_PASS, t0 * P : t1 * P].rearrange("(p j) c -> p j c", j=PACK)
            )
            for t in range(t0, t1):
                w1_raw[z, t] = raw[:, :, (t - t0) * P : (t - t0 + 1) * P]

        load_w1(0, 0, 1)
        load_words(1)
        load_w1(1, 0, 1)
        nc.sync.dma_start(lists[2][:], pos2)
        nc.sync.dma_start(lists[0][:], cen)
        for z in range(PASSES):
            load_w1(z, 1, 2)
        gate_sb = keep.tile([P, 2, V], F32, name="gate_sb")
        nc.sync.dma_start(gate_sb[:], gate.rearrange("d p v -> p d v"))
        for z in range(PASSES):
            load_w1(z, 2, 4)
        w2_raw = keep.tile([P, PACK, N], F32, name="w2_raw")
        nc.sync.dma_start(w2_raw[:], w2.rearrange("(p j) n -> p j n", j=PACK))

        ident = keep.tile([P, P], F32, name="ident")
        make_identity(nc, ident[:])

        def interleave(dst, raw, copy=nc.scalar.copy):
            copy(
                dst.rearrange("p (c i j) -> p c j i", i=4, j=PACK),
                raw.rearrange("p j (c i) -> p c j i", i=4),
            )

        def quantize(codes, scales, grouped):
            nc.vector.quantize_mx(out=codes.bitcast(FP8X4), scales=scales, in_=grouped)

        codes_all = [keep.tile([P, n * PASSES * P], U32, name=f"w1_codes{t}", align_bytes=64) for t, n in enumerate((1, 1))]
        scales_all = [keep.tile([P, n * PASSES * P], U8, name=f"w1_scales{t}", align_bytes=64) for t, n in enumerate((1, 1, 1, 1))]
        w1_codes = codes_all
        w1_scales = scales_all

        x_scale = keep.tile([P, S], U8, name="x_scale", align_bytes=64)
        x_first = keep.tile([P, S], U32, name="x_first", align_bytes=64)
        nc.vector.tensor_copy(x_first[:], word_win[0][:].indirect(offs_sb[:]))
        nc.vector.tensor_copy(x_scale[:], scale_win[:].indirect(offs_sb[:]))

        def prepare_first(z):
            grouped = keep.tile([P, K_PASS], BF16, name=f"w1_first{z}", tag=f"w1_first{z}", align_bytes=64)
            interleave(grouped[:], w1_raw[z, 0])
            quantize(w1_codes[0][:, z * P : (z + 1) * P], w1_scales[0][:, z * P : (z + 1) * P], grouped[:])

        pieces = [(0, 512), (512, 768), (768, 1024)]
        x_low = keep.tile([P, BANK], U32, name="x_low", align_bytes=64)
        x_later = []

        def words(z, a, b):
            if z == 0:
                return x_first[:, a:b]
            return x_low[:, a:b] if b <= BANK else x_later[0][:, a - BANK : b - BANK]

        h = [keep.tile([P, S], F32, name=f"h{t}", tag=f"h{t}", align_bytes=64) for t in range(TILES)]

        def bank_tile(n):
            return psum.tile([P, BANK], F32, name="bank", tag=f"bank{n}")

        def project(t, a, b, n):
            acc = bank_tile(n)
            for z in range(PASSES):
                nc.tensor.matmul_mx(
                    out=acc[:, : b - a],
                    lhsT=w1_codes[t][:, z * P : (z + 1) * P].bitcast(FP8X4),
                    lhsT_scale=w1_scales[t][:, z * P : (z + 1) * P],
                    rhs=words(z, a, b).bitcast(FP8X4),
                    rhs_scale=x_scale[4 * z :, a:b],
                    start=(z == 0),
                    stop=(z == PASSES - 1),
                )
            nc.scalar.copy(h[t][:, a:b], acc[:, : b - a])

        prepare_first(0)
        for n, (a, b) in enumerate(pieces):
            nc.vector.tensor_copy(words(1, a, b), word_win[1][:].indirect(entries(offs_sb, a, b)))
            if n == 0:
                prepare_first(1)
                x_later.append(keep.tile([P, BANK], U32, name="x_high", tag="w1_first1", align_bytes=64))
            project(0, a, b, n)

        neg_gate = keep.tile([P, 2, V], F32, name="neg_gate")
        nc.scalar.mul(neg_gate[:], gate_sb[:], -1.0)

        z_rows = keep.tile([P, V // P, H], BF16, name="z_rows", tag="w1_raw1_2", align_bytes=64)

        def prepare(ts, banks, tag, copy):
            grouped = keep.tile([P, len(ts), PASSES, K_PASS], BF16, name="w1_grouped", tag=tag, align_bytes=64)
            for n, t in enumerate(ts):
                for z in range(PASSES):
                    interleave(grouped[:, n, z, :], w1_raw[z, t], copy)
            if ts[0] > 1:
                codes_all.append(keep.tile([P, PASSES * P], U32, name="late_codes", tag=("h0" if ts[0] == 2 else "term1_0_0"), align_bytes=64))
            quantize(codes_all[ts[0]][:], scales_all[ts[0]][:], grouped[:].rearrange("p n z c -> p (n z c)"))
            for n, t in enumerate(ts):
                for half in range(2):
                    project(t, half * BANK, (half + 1) * BANK, banks[2 * n + half])

        ring = keep.tile([P, 6 * P], F32, name="ring", align_bytes=64)

        def look_up(t, a, b, n, between=(), place=None):
            width = b - a
            bank = bank_tile(n)
            for d in range(3):
                if place is None:
                    term = keep.tile([P, width], F32, name="term", tag=f"term{t}_{a}_{d}", align_bytes=64)[:]
                else:
                    term = ring[:, place + d * width : place + (d + 1) * width]
                window = h[t][:].indirect(entries(lists[d], a, b))
                if d == 0:
                    nc.vector.tensor_copy(term, window)
                else:
                    nc.vector.tensor_tensor(term, window, neg_gate[:, d - 1, a:b], MULT)
                for c in range(0, width, P):
                    nc.tensor.matmul(
                        bank[:, c : c + P], term[:, c : c + P], ident[:], is_transpose=True,
                        start=(d == 0 and c == 0), stop=(d == 2 and c == width - P),
                    )
                if d < len(between):
                    prepare(*between[d])
            nc.scalar.copy(
                z_rows[:, a // P : b // P, :].rearrange("v c (u p e) -> v c u p e", u=2, e=2)[:, :, :, 32 * t : 32 * t + 32, :],
                bank[:, :width].rearrange("v (c p u e) -> v c u p e", p=32, u=2, e=2),
            )

        def turn_back(a, b, n, tag):
            width = b - a
            bank = bank_tile(n)
            pairs = z_rows[:, a // P : b // P, :].rearrange("v c i -> v (c i)").bitcast(F32)
            for c in range(0, 2 * width, P):
                nc.tensor.transpose(bank[:, c : c + P], pairs[:, c : c + P], ident[:])
            grouped = keep.tile([P, PACK * width], BF16, name="z_grouped", tag=tag, align_bytes=64)
            nc.scalar.copy(
                grouped[:].bitcast(F32).rearrange("p (c v u) -> p c v u", v=P, u=2),
                bank[:, : 2 * width].rearrange("p (c u v) -> p c v u", v=P, u=2),
            )
            return grouped

        def finish(grouped, a, b, n, copy_out, tag):
            width = b - a
            codes = keep.tile([P, width], U32, name=f"z_codes{a}", tag=tag, align_bytes=64)
            scales = keep.tile([P, width], U8, name=f"z_scales{a}", align_bytes=64)
            quantize(codes[:], scales[:], grouped[:])
            acc = bank_tile(n)
            nc.tensor.matmul_mx(
                out=acc[:, :width], lhsT=w2_codes[:].bitcast(FP8X4), lhsT_scale=w2_scales[:],
                rhs=codes[:].bitcast(FP8X4), rhs_scale=scales[:], start=True, stop=True,
            )
            result = keep.tile([P, width], F32, name=f"result{a}")
            copy_out(result[:], acc[:, :width])
            nc.sync.dma_start(out[:, a:b], result[:])

        prepare([1], (3, 0), "term0_0_0", nc.vector.tensor_copy)
        look_up(0, 0, V, 4)
        prepare([2], (1, 2), "term1_0_0", nc.scalar.copy)
        look_up(1, 0, 384, 5, [([3], (3, 0), "term1_0_2", nc.scalar.copy)])
        look_up(2, 0, 256, 6, place=0)
        w2_grouped = keep.tile([P, PACK * N], BF16, name="w2_grouped", tag="w2_grouped", align_bytes=64)
        interleave(w2_grouped[:], w2_raw[:])
        look_up(3, 0, 256, 7, place=0)
        first = turn_back(0, 256, 1, "first_grouped")
        look_up(2, 256, 384, 4, place=0)
        look_up(3, 256, 384, 7, place=384)
        second = turn_back(256, 384, 2, "second")
        look_up(1, 384, 512, 1, place=0)
        look_up(2, 384, 512, 7, place=384)
        look_up(3, 384, 512, 1, place=0)
        w2_codes = keep.tile([P, N], U32, name="w2_codes", tag="h3", align_bytes=64)
        w2_scales = keep.tile([P, N], U8, name="w2_scales", align_bytes=64)
        quantize(w2_codes[:], w2_scales[:], w2_grouped[:])
        finish(first, 0, 256, 0, nc.vector.tensor_copy, "w2_grouped")
        third = turn_back(384, 512, 3, "third")
        finish(second, 256, 384, 6, nc.vector.tensor_copy, "codes1")
        finish(third, 384, 512, 5, nc.vector.tensor_copy, "codes2")
